import numpy as np
import ml_dtypes


def mxq(x, axis, fmt="e4m3"):
    dtype, down = {"e4m3": (ml_dtypes.float8_e4m3fn, 7), "e5m2": (ml_dtypes.float8_e5m2, 14)}[fmt]
    v = np.moveaxis(np.asarray(x, np.float32).astype(ml_dtypes.bfloat16).astype(np.float64), axis, -1)
    blocks = v.reshape(v.shape[:-1] + (-1, 32))
    amax = np.abs(blocks).max(-1, keepdims=True)
    byte = np.maximum(np.where(amax > 0, np.frexp(amax)[1] - 1 + 127, 0) - down, 1)
    scale = np.exp2(byte - 127.0)
    codes = (blocks / scale).astype(np.float32).astype(dtype).astype(np.float64)
    return np.moveaxis((codes * scale).reshape(v.shape), -1, axis)


WIDE = False


def mx_kscale(k):
    if not WIDE:
        return np.ones(k)
    levels = np.array([30, -30])
    if k % 512:
        return np.exp2(np.random.permutation(np.resize(levels, k // 32))).repeat(32)
    a = np.empty((k // 512, 16))
    for p in range(k // 512):
        a[p, :8] = np.random.permutation(np.resize(levels, 8))
        for g in range(8):
            far = levels[np.abs(levels - a[p, g]) >= 10]
            a[p, g + 8] = far[np.random.randint(len(far))]
    return np.exp2(a.ravel()).repeat(32)


def f64(x):
    return np.asarray(x).astype(np.float64)


def striped(idx):
    return np.tile(np.asarray(idx).reshape(-1, 16).T, (8, 1)).astype(np.uint16)


def unstriped(offs):
    return offs[:16].T.reshape(-1).astype(np.int64)


E2M1 = np.array([0.0, 0.5, 1.0, 1.5, 2.0, 3.0, 4.0, 6.0, -0.0, -0.5, -1.0, -1.5, -2.0, -3.0, -4.0, -6.0])


def pack_weight(w, fmt):
    k, n = w.shape
    w = f64(np.asarray(w, np.float32).astype(ml_dtypes.bfloat16)).reshape(k // 32, 32, n)
    amax = np.abs(w).max(1)
    if fmt == "e4m3":
        byte = np.frexp(amax)[1] - 1 + 127 - 7
    else:
        mant, ex = np.frexp(amax / 6.0)
        byte = np.where(mant > 0.5, ex, ex - 1) + 127
    byte = np.clip(np.where(amax > 0, byte, 1), 1, 254)
    scaled = (w * np.exp2(127.0 - byte)[:, None, :]).reshape(k, n).astype(np.float32)
    by_word = np.ascontiguousarray(scaled.reshape(k // 512, 128, 4, n).transpose(0, 1, 3, 2))
    if fmt == "e4m3":
        words = by_word.astype(ml_dtypes.float8_e4m3fn).view(np.uint8)
    else:
        c = by_word.astype(ml_dtypes.float4_e2m1fn).view(np.uint8) & 0xF
        words = (c[..., 0::2] | (c[..., 1::2] << 4)).reshape(k // 512, 128, 2 * n)
    return np.ascontiguousarray(words), np.ascontiguousarray(byte.astype(np.uint8).reshape(k // 512, 16, n))


def unpack_weight(words, scales, fmt):
    g, _, n = scales.shape
    words = np.ascontiguousarray(words).reshape(g, 128, n, -1)
    if fmt == "e4m3":
        vals = words.view(ml_dtypes.float8_e4m3fn).astype(np.float64)
    else:
        nib = np.empty((g, 128, n, 4), np.uint8)
        nib[..., 0::2] = words & 0xF
        nib[..., 1::2] = words >> 4
        vals = E2M1[nib]
    vals = vals * np.repeat(np.exp2(scales.astype(np.float64) - 127.0), 8, axis=1)[..., None]
    return vals.transpose(0, 1, 3, 2).reshape(g * 512, n)


K, T, J, N = 1024, 1024, 256, 256


def setup_inputs():
    n = np.random.standard_normal
    idx = np.random.permutation(T)[:J]
    fk = mx_kscale(K)
    xtp = pack_weight(n((K, T)) * np.random.uniform(0.4, 1.6, (1, T)) / fk[:, None], "e2m1")
    wap = pack_weight(n((K, N)) * 1 / np.sqrt(K) * fk[:, None], "e2m1")
    return {
        "xt_words": xtp[0],
        "xt_scales": xtp[1],
        "wa_words": wap[0],
        "wa_scales": wap[1],
        "wb": (n((K, N)) * 1 / np.sqrt(K) * fk[:, None]).astype(np.float32),
        "bi": (np.random.uniform(-0.6, 0.6, (1, N))).astype(np.float32),
        "gm": (np.random.uniform(0.5, 2.0, (1, N))).astype(np.float32),
        "offs": striped(idx),
    }


def reference(xt_words, xt_scales, wa_words, wa_scales, wb, bi, gm, offs):
    idx = unstriped(offs)
    xtu = unpack_weight(xt_words, xt_scales, "e2m1")
    wau = unpack_weight(wa_words, wa_scales, "e2m1")
    xtidxg = xtu[:, idx]
    a = xtidxg.T @ wau
    wbq = mxq(f64(wb), 0, "e5m2")
    b0 = xtidxg.T @ wbq
    b2 = b0 + f64(bi)
    mb = np.mean(np.abs(b2), axis=1, keepdims=True)
    y = np.maximum(a - mb, 0.0) * f64(gm)
    return y

from contextlib import ExitStack

import concourse.mybir as mybir
from concourse.masks import make_identity

K, T, J, N = 1024, 1024, 256, 256
FLOPS = 2 * 2 * K * J * N

F32 = mybir.dt.float32
BF16 = mybir.dt.bfloat16
I32 = mybir.dt.int32
U32 = mybir.dt.uint32
U16 = mybir.dt.uint16
U8 = mybir.dt.uint8
FP4X4 = mybir.dt.float4_e2m1fn_x4
E5M2X4 = mybir.dt.float8_e5m2_x4
ALU = mybir.AluOpType
ACT = mybir.ActivationFunctionType

P = 128
PACK = 4
PASSES = K // (P * PACK)
TILES = J // P
WB_PIECES = ((0, 0, 256, 160), (1, 0, 128, 0), (1, 128, 128, 88))


def tile_list_rows_onetoken_abovemean_kernel(tc, xt_words, xt_scales, wa_words, wa_scales, wb, bi, gm, offs, out):
    nc = tc.nc
    with ExitStack() as ctx:
        sb = ctx.enter_context(tc.tile_pool(name="sb", bufs=1))
        ps = ctx.enter_context(tc.psum_pool(name="ps", bufs=1))

        offsets = sb.tile([P, J // 16], U16, name="offsets")
        nc.sync.dma_start(offsets[:], offs)

        def load_scale_rows(plane, scales):
            nc.vector.memset(plane[:].bitcast(I32), 0)
            for q in range(4):
                nc.sync.dma_start(
                    plane[32 * q : 32 * q + 4, :].bitcast(I32).rearrange("r (z c) -> r z c", z=PASSES),
                    scales[:, 4 * q : 4 * q + 4, :].bitcast(I32).rearrange("z r c -> r z c"),
                )

        def load_words(z):
            words = sb.tile([P, T], U16, name=f"xw{z}", align_bytes=64)
            nc.sync.dma_start(words[:].bitcast(I32), xt_words[z].bitcast(I32))
            return words

        xw = [load_words(0)]
        xs = sb.tile([P, PASSES * T], U8, name="xs", align_bytes=64)
        load_scale_rows(xs, xt_scales)
        xw.append(load_words(1))

        wb_raw = []
        for s, (z, first, width, share) in enumerate(WB_PIECES):
            raw = sb.tile([P, PACK, width], F32, name=f"wb_raw{s}", align_bytes=64)
            rows = wb[z * P * PACK : (z + 1) * P * PACK, first : first + width]
            nc.sync.dma_start(raw[:], rows.rearrange("(p t) n -> p t n", t=PACK))
            wb_raw.append(raw)
            if s == 0:
                bi_cols = sb.tile([P, 2], F32, name="bi_cols")
                gm_cols = sb.tile([P, 2], F32, name="gm_cols")
                nc.sync.dma_start(bi_cols[:], bi.rearrange("o (p c) -> (o p) c", c=2))
                nc.sync.dma_start(gm_cols[:], gm.rearrange("o (p c) -> (o p) c", c=2))

        waw = sb.tile([P, PASSES, 2 * N], U8, name="waw", align_bytes=64)
        nc.sync.dma_start(waw[:].bitcast(I32), wa_words.bitcast(I32).rearrange("z p c -> p z c"))
        was = sb.tile([P, PASSES * N], U8, name="was", align_bytes=64)
        load_scale_rows(was, wa_scales)

        ident = sb.tile([P, P], F32, name="ident")
        make_identity(nc, ident[:])

        bi_ps = ps.tile([P, 2, P], F32, name="bi_ps")
        gm_ps = ps.tile([P, 2, P], F32, name="gm_ps")
        for cols, spread in ((bi_cols, bi_ps), (gm_cols, gm_ps)):
            for c in range(2):
                nc.tensor.transpose(spread[:, c, :], cols[:, c : c + 1].to_broadcast([P, P]), ident[:])
        bi_rows = sb.tile([P, N], F32, name="bi_rows")
        nc.scalar.copy(bi_rows[:].rearrange("p (k c) -> p k c", c=2), bi_ps[:].rearrange("p c k -> p k c"))

        def gather(name, dtype, window):
            picked = sb.tile([P, J], dtype, name=name, align_bytes=64)
            nc.vector.tensor_copy(picked[:], window.indirect(offsets[:]))
            return picked

        gw = [gather("gw0", U16, xw[0][:])]
        gs = [gather(f"gs{z}", U8, xs[:, z * T : (z + 1) * T]) for z in range(PASSES)]
        gw.append(gather("gw1", U16, xw[1][:]))

        b_ps = [ps.tile([P, N], F32, name=f"b_ps{i}") for i in range(TILES)]
        a_ps = [ps.tile([P, N], F32, name=f"a_ps{i}") for i in range(TILES)]
        for s, (z, first, width, share) in enumerate(WB_PIECES):
            grouped = sb.tile([P, width, PACK], BF16, name=f"grouped{s}", tag="grouped", bufs=2, align_bytes=64)
            for copy, cols in ((nc.scalar.copy, slice(share, width)), (nc.vector.tensor_copy, slice(0, share))):
                if cols.stop > cols.start:
                    copy(
                        grouped[:, cols, :].rearrange("p (c i) t -> p c t i", i=4),
                        wb_raw[s][:, :, cols].rearrange("p t (c i) -> p c t i", i=4),
                    )
            codes = sb.tile([P, width], U32, name=f"wbq{s}", align_bytes=64)
            scales = sb.tile([P, width], U8, name=f"wbs{s}", align_bytes=64)
            nc.vector.quantize_mx(out=codes[:].bitcast(E5M2X4), scales=scales[:], in_=grouped[:].rearrange("p n t -> p (n t)"))
            for i in range(TILES):
                slots = slice(i * P, (i + 1) * P)
                nc.tensor.matmul_mx(
                    out=b_ps[i][:, first : first + width],
                    lhsT=gw[z][:, slots].bitcast(FP4X4),
                    lhsT_scale=gs[z][:, slots],
                    rhs=codes[:].bitcast(E5M2X4),
                    rhs_scale=scales[:],
                    start=(s == 0),
                    stop=(s == len(WB_PIECES) - 1),
                )
        for i in range(TILES):
            slots = slice(i * P, (i + 1) * P)
            for z in range(PASSES):
                nc.tensor.matmul_mx(
                    out=a_ps[i][:],
                    lhsT=gw[z][:, slots].bitcast(FP4X4),
                    lhsT_scale=gs[z][:, slots],
                    rhs=waw[:, z, :].bitcast(FP4X4),
                    rhs_scale=was[:, z * N : (z + 1) * N],
                    start=(z == 0),
                    stop=(z == PASSES - 1),
                )

        b2, mb, above = [], [], []
        for i in range(TILES):
            biased = sb.tile([P, N], F32, name=f"b2_{i}")
            nc.vector.tensor_tensor(biased[:], b_ps[i][:], bi_rows[:], ALU.add)
            b2.append(biased)
        for i in range(TILES):
            magnitude = sb.tile([P, N], F32, name=f"magnitude{i}")
            mean = sb.tile([P, 1], F32, name=f"mb{i}")
            nc.scalar.activation(magnitude[:], b2[i][:], ACT.Abs, scale=1.0 / N, accum_out=mean[:])
            mb.append(mean)
        for i in range(TILES):
            kept = sb.tile([P, N], F32, name=f"above{i}")
            nc.vector.tensor_scalar(kept[:], a_ps[i][:], mb[i][:], 0.0, ALU.subtract, ALU.max)
            above.append(kept)
        for i, queue in zip(range(TILES), (nc.sync, nc.scalar)):
            y = sb.tile([P, N], F32, name=f"y{i}")
            nc.vector.tensor_tensor(
                y[:].rearrange("p (k c) -> p k c", c=2),
                above[i][:].rearrange("p (k c) -> p k c", c=2),
                gm_ps[:].rearrange("p c k -> p k c"),
                ALU.mult,
            )
            queue.dma_start(out[i * P : (i + 1) * P, :], y[:])
